import numpy as np
import ml_dtypes


def mxq(x, axis, fmt="e4m3"):
    dtype, down = {"e4m3": (ml_dtypes.float8_e4m3fn, 7), "e5m2": (ml_dtypes.float8_e5m2, 14)}[fmt]
    v = np.moveaxis(np.asarray(x, np.float32).astype(ml_dtypes.bfloat16).astype(np.float64), axis, -1)
    blocks = v.reshape(v.shape[:-1] + (-1, 32))
    amax = np.abs(blocks).max(-1, keepdims=True)
    byte = np.maximum(np.where(amax > 0, np.frexp(amax)[1] - 1 + 127, 0) - down, 1)
    scale = np.exp2(byte - 127.0)
    codes = (blocks / scale).astype(np.float32).astype(dtype).astype(np.float64)
    return np.moveaxis((codes * scale).reshape(v.shape), -1, axis)


WIDE = False


def mx_kscale(k):
    if not WIDE:
        return np.ones(k)
    levels = np.array([10, -10, 5, -5, 0])
    if k % 512:
        return np.exp2(np.random.permutation(np.resize(levels, k // 32))).repeat(32)
    a = np.empty((k // 512, 16))
    for p in range(k // 512):
        a[p, :8] = np.random.permutation(np.resize(levels, 8))
        for g in range(8):
            far = levels[np.abs(levels - a[p, g]) >= 10]
            a[p, g + 8] = far[np.random.randint(len(far))]
    return np.exp2(a.ravel()).repeat(32)


def f64(x):
    return np.asarray(x).astype(np.float64)


def striped(idx):
    return np.tile(np.asarray(idx).reshape(-1, 16).T, (8, 1)).astype(np.uint16)


def unstriped(offs):
    return offs[:16].T.reshape(-1).astype(np.int64)


E2M1 = np.array([0.0, 0.5, 1.0, 1.5, 2.0, 3.0, 4.0, 6.0, -0.0, -0.5, -1.0, -1.5, -2.0, -3.0, -4.0, -6.0])


def pack_weight(w, fmt):
    k, n = w.shape
    w = f64(np.asarray(w, np.float32).astype(ml_dtypes.bfloat16)).reshape(k // 32, 32, n)
    amax = np.abs(w).max(1)
    if fmt == "e4m3":
        byte = np.frexp(amax)[1] - 1 + 127 - 7
    else:
        mant, ex = np.frexp(amax / 6.0)
        byte = np.where(mant > 0.5, ex, ex - 1) + 127
    byte = np.clip(np.where(amax > 0, byte, 1), 1, 254)
    scaled = (w * np.exp2(127.0 - byte)[:, None, :]).reshape(k, n).astype(np.float32)
    by_word = np.ascontiguousarray(scaled.reshape(k // 512, 128, 4, n).transpose(0, 1, 3, 2))
    if fmt == "e4m3":
        words = by_word.astype(ml_dtypes.float8_e4m3fn).view(np.uint8)
    else:
        c = by_word.astype(ml_dtypes.float4_e2m1fn).view(np.uint8) & 0xF
        words = (c[..., 0::2] | (c[..., 1::2] << 4)).reshape(k // 512, 128, 2 * n)
    return np.ascontiguousarray(words), np.ascontiguousarray(byte.astype(np.uint8).reshape(k // 512, 16, n))


def unpack_weight(words, scales, fmt):
    g, _, n = scales.shape
    words = np.ascontiguousarray(words).reshape(g, 128, n, -1)
    if fmt == "e4m3":
        vals = words.view(ml_dtypes.float8_e4m3fn).astype(np.float64)
    else:
        nib = np.empty((g, 128, n, 4), np.uint8)
        nib[..., 0::2] = words & 0xF
        nib[..., 1::2] = words >> 4
        vals = E2M1[nib]
    vals = vals * np.repeat(np.exp2(scales.astype(np.float64) - 127.0), 8, axis=1)[..., None]
    return vals.transpose(0, 1, 3, 2).reshape(g * 512, n)


def sigmoid(v):
    return 1.0 / (1.0 + np.exp(-v))


D, K, R, T, I, Q = 512, 512, 512, 2048, 512, 128


def setup_inputs():
    n = np.random.standard_normal
    idx = np.random.permutation(T)[:I]
    fd = mx_kscale(D)
    fk = mx_kscale(K)
    fi = mx_kscale(I)
    keysp = pack_weight(n((D, T)) / fd[:, None], "e4m3")
    tabp = pack_weight(n((K, T)) / fk[:, None], "e4m3")
    return {
        "query": (n((D, Q)) * 0.6 / np.sqrt(D) * fd[:, None]).astype(np.float32),
        "query2": (n((D, Q)) * 1.0 / np.sqrt(D) * fd[:, None]).astype(np.float32),
        "keys_words": keysp[0],
        "keys_scales": keysp[1],
        "tab_words": tabp[0],
        "tab_scales": tabp[1],
        "w1": (n((K, R)) * 1 / np.sqrt(K) * fk[:, None]).astype(np.float32),
        "gain": (np.random.uniform(0.5, 2.0, (R, 1))).astype(np.float32),
        "os": (np.random.uniform(4.0, 16.0, (1, I)) * fi).astype(np.float32),
        "vs": (np.random.uniform(0.5, 2.0, (1, I)) / fi).astype(np.float32),
        "offs": striped(idx),
    }


def reference(query, query2, keys_words, keys_scales, tab_words, tab_scales, w1, gain, os, vs, offs):
    idx = unstriped(offs)
    keysu = unpack_weight(keys_words, keys_scales, "e4m3")
    tabu = unpack_weight(tab_words, tab_scales, "e4m3")
    queryq = mxq(f64(query), 0, "e4m3")
    keysidxg = keysu[:, idx]
    a = queryq.T @ keysidxg
    query2q = mxq(f64(query2), 0, "e4m3")
    b = query2q.T @ keysidxg
    p = np.exp(a - np.max(a, axis=1, keepdims=True)) * sigmoid(b)
    z = np.sum(p, axis=1, keepdims=True)
    w = p / z
    w1q = mxq(f64(w1), 0, "e4m3")
    tabidxg = tabu[:, idx]
    zh = w1q.T @ tabidxg
    ht = np.tanh(zh)
    hv = ht * f64(gain)
    wo1 = w * f64(os)
    wt1 = wo1.T
    hw = hv * f64(vs)
    ht1 = hw.T
    wt1q = mxq(wt1, 0, "e4m3")
    ht1q = mxq(ht1, 0, "e4m3")
    o = wt1q.T @ ht1q
    return o

@@ -1,0 +1,186 @@
+from contextlib import ExitStack
+
+import concourse.mybir as mybir
+from concourse.masks import make_identity
+
+D, K, R, T, I, Q = 512, 512, 512, 2048, 512, 128
+FLOPS = 2 * (2 * D * Q * I + K * R * I + I * Q * R)
+
+F32 = mybir.dt.float32
+BF16 = mybir.dt.bfloat16
+I32 = mybir.dt.int32
+U32 = mybir.dt.uint32
+U16 = mybir.dt.uint16
+U8 = mybir.dt.uint8
+FP8X4 = mybir.dt.float8_e4m3fn_x4
+ACT = mybir.ActivationFunctionType
+ALU = mybir.AluOpType
+
+P = 128
+PACK = 4
+R_TILES = R // P
+W1_LOADS = 2
+CAST_ON_VECTOR = (0, 1)
+
+
+def tile_attend_lrgained_asked_kernel(tc, query, query2, keys_words, keys_scales, tab_words, tab_scales,
+                                       w1, gain, slot_factor, vs, offs, out):
+    nc = tc.nc
+    with ExitStack() as ctx:
+        sb = ctx.enter_context(tc.tile_pool(name="sb", bufs=1))
+        ring = ctx.enter_context(tc.tile_pool(name="ring", bufs=2))
+        ps = ctx.enter_context(tc.psum_pool(name="ps", bufs=1))
+        ps2 = ctx.enter_context(tc.psum_pool(name="ps2", bufs=2))
+
+        def load_words(name, words):
+            window = sb.tile([P, T], U32, name=name, align_bytes=64)
+            nc.sync.dma_start(out=window[:].bitcast(I32), in_=words[0].rearrange("p n t -> p (n t)").bitcast(I32))
+            return window
+
+        def load_scales(window, scales):
+            for row in range(4):
+                nc.sync.dma_start(out=window[row:P:32, :].bitcast(I32), in_=scales[0, row:16:4, :].bitcast(I32))
+
+        def gather(name, window, dtype):
+            picked = sb.tile([P, I], dtype, name=name, align_bytes=64)
+            nc.vector.tensor_copy(out=picked[:], in_=window[:].indirect(offsets[:]))
+            return picked
+
+        def interleave(engine_copy, grouped, raw):
+            engine_copy(out=grouped.rearrange("p (c i) t -> p c t i", i=4), in_=raw.rearrange("p t (c i) -> p c t i", i=4))
+
+        def quantize(codes, scales, grouped):
+            nc.vector.quantize_mx(out=codes.bitcast(FP8X4), scales=scales, in_=grouped)
+
+        def product(bank, lhs, lhs_scales, rhs, rhs_scales):
+            nc.tensor.matmul_mx(out=bank, lhsT=lhs.bitcast(FP8X4), lhsT_scale=lhs_scales, rhs=rhs.bitcast(FP8X4),
+                                rhs_scale=rhs_scales, start=True, stop=True)
+
+        def turn_slots(name, values, grouped):
+            words = values.bitcast(F32)
+            turned = ps2.tile([P, 2, P], F32, name="turned")
+            for u in range(2):
+                nc.tensor.transpose(turned[:, u, :], words[:, u * P:(u + 1) * P], ident[:])
+            nc.scalar.copy(out=grouped.bitcast(F32).rearrange("p (c u) -> p c u", u=2), in_=turned[:].rearrange("p u c -> p c u"))
+
+        key_scale_window = sb.tile([P, T], U8, align_bytes=64)
+        tab_scale_window = sb.tile([P, T], U8, align_bytes=64)
+        nc.vector.memset(key_scale_window[:].bitcast(I32), 0)
+        nc.vector.memset(tab_scale_window[:].bitcast(I32), 0)
+
+        offsets = sb.tile([P, I // 16], U16)
+        nc.sync.dma_start(offsets[:], offs)
+        q2_raw = sb.tile([P, PACK, Q], F32)
+        nc.sync.dma_start(out=q2_raw[:], in_=query2.rearrange("(p t) q -> p t q", t=PACK))
+        q_raw = sb.tile([P, PACK, Q], F32)
+        nc.sync.dma_start(out=q_raw[:], in_=query.rearrange("(p t) q -> p t q", t=PACK))
+        load_scales(key_scale_window, keys_scales)
+        key_window = load_words("key_window", keys_words)
+        load_scales(tab_scale_window, tab_scales)
+        tab_window = load_words("tab_window", tab_words)
+        w1_cols = R // W1_LOADS
+        w1_raw = []
+        for h in range(W1_LOADS):
+            part = sb.tile([P, PACK, w1_cols], F32, name="w1_raw%d" % h)
+            nc.sync.dma_start(out=part[:], in_=w1[:, h * w1_cols:(h + 1) * w1_cols].rearrange("(p t) r -> p t r", t=PACK))
+            w1_raw.append(part)
+
+        ident = sb.tile([P, P], F32)
+        make_identity(nc, ident[:])
+        os_col = sb.tile([P, PACK], F32)
+        nc.gpsimd.dma_start(out=os_col[:], in_=slot_factor.rearrange("o (p t) -> p (o t)", t=PACK))
+        vs_col = sb.tile([P, PACK], F32)
+        nc.gpsimd.dma_start(out=vs_col[:], in_=vs.rearrange("o (p t) -> p (o t)", t=PACK))
+        gain_col = sb.tile([P, R_TILES], F32)
+        with nc.allow_non_contiguous_dma(reason="one gain a partition"):
+            nc.gpsimd.dma_start(out=gain_col[:], in_=gain.rearrange("(j m) o -> m (j o)", m=P))
+
+        warm = sb.tile([P, 1], F32)
+        nc.scalar.activation(out=warm[:], in_=ident[:, 0:1], func=ACT.Sigmoid)
+
+        os_rows = sb.tile([P, I], F32)
+        vs_rows = sb.tile([P, I], F32)
+        for rows, col in ((os_rows, os_col), (vs_rows, vs_col)):
+            spread = ps.tile([P, PACK, P], F32, name="spread")
+            for t in range(PACK):
+                nc.tensor.transpose(spread[:, t, :], col[:, t:t + 1].to_broadcast([P, P]), ident[:])
+            nc.scalar.copy(out=rows[:].rearrange("m (u s e) -> m u s e", u=2, e=2), in_=spread[:].rearrange("m (u e) s -> m u s e", u=2))
+
+        def dealt(bank):
+            return bank.rearrange("m (s u e) -> m u s e", u=2, e=2)
+
+        def placed(tile):
+            return tile.rearrange("m (u s e) -> m u s e", u=2, e=2)
+
+        key_scales = gather("key_scales", key_scale_window, U8)
+
+        q_grouped = sb.tile([P, 2 * Q, PACK], BF16, align_bytes=64)
+        interleave(nc.scalar.copy, q_grouped[:, Q:, :], q2_raw[:])
+        interleave(nc.scalar.copy, q_grouped[:, :Q, :], q_raw[:])
+        q_codes = sb.tile([P, 2 * Q], U32, align_bytes=64)
+        q_scales = sb.tile([P, 2 * Q], U8, align_bytes=64)
+        quantize(q_codes[:], q_scales[:], q_grouped[:].rearrange("p c t -> p (c t)"))
+
+        keys = gather("keys", key_window, U32)
+        b_bank = ps.tile([P, I], F32, tag="bank_b")
+        product(b_bank[:], q_codes[:, Q:], q_scales[:, Q:], keys[:], key_scales[:])
+        a_bank = ps.tile([P, I], F32, tag="bank_a")
+        product(a_bank[:], q_codes[:, :Q], q_scales[:, :Q], keys[:], key_scales[:])
+
+        gate = sb.tile([P, I], F32)
+        nc.scalar.activation(out=placed(gate[:]), in_=dealt(b_bank[:]), func=ACT.Sigmoid)
+        tab_scales_g = gather("tab_scales_g", tab_scale_window, U8)
+        neg_max = sb.tile([P, 1], F32)
+        nc.vector.tensor_reduce(out=neg_max[:], in_=a_bank[:], axis=mybir.AxisListType.X, op=ALU.max, negate=True)
+        expo = sb.tile([P, I], F32)
+        nc.scalar.activation(out=placed(expo[:]), in_=dealt(a_bank[:]), func=ACT.Exp, bias=neg_max[:])
+        tab = gather("tab", tab_window, U32)
+
+        prob = sb.tile([P, I], F32)
+        total = sb.tile([P, 1], F32)
+        nc.vector.scalar_tensor_tensor(out=prob[:], in0=expo[:], scalar=1.0, in1=gate[:], op0=ALU.mult, op1=ALU.mult,
+                                       accum_out=total[:])
+        inv_total = sb.tile([P, 1], F32)
+        nc.vector.reciprocal(out=inv_total[:], in_=total[:])
+        weights = sb.tile([P, I], BF16, align_bytes=64)
+        nc.vector.scalar_tensor_tensor(out=weights[:], in0=prob[:], scalar=inv_total[:], in1=os_rows[:], op0=ALU.mult, op1=ALU.mult)
+        wt_grouped = sb.tile([P, Q * PACK], BF16, align_bytes=64)
+        turn_slots("wt", weights[:], wt_grouped[:])
+        wt_codes = sb.tile([P, Q], U32, align_bytes=64)
+        wt_scales = sb.tile([P, Q], U8, align_bytes=64)
+        quantize(wt_codes[:], wt_scales[:], wt_grouped[:])
+
+        per_load = R_TILES // W1_LOADS
+        groups = ((0, 1), (2,), (3,))
+        ht_codes = [sb.tile([P, len(g) * P], U32, name="ht_codes%d" % n, align_bytes=64) for n, g in enumerate(groups)]
+        ht_scales = [sb.tile([P, len(g) * P], U8, name="ht_scales%d" % n, align_bytes=64) for n, g in enumerate(groups)]
+        w1_codes = []
+        w1_scales = []
+        for j in range(R_TILES):
+            cols = slice((j % per_load) * P, (j % per_load + 1) * P)
+            w1_grouped = sb.tile([P, P, PACK], BF16, name="w1_grouped%d" % j, align_bytes=64)
+            interleave(nc.vector.tensor_copy if j in CAST_ON_VECTOR else nc.scalar.copy, w1_grouped[:], w1_raw[j // per_load][:, :, cols])
+            w1_codes.append(sb.tile([P, P], U32, name="w1_codes%d" % j, align_bytes=64))
+            w1_scales.append(sb.tile([P, P], U8, name="w1_scales%d" % j, align_bytes=64))
+            quantize(w1_codes[j][:], w1_scales[j][:], w1_grouped[:].rearrange("p c t -> p (c t)"))
+
+        for j in range(R_TILES):
+            zh = ps2.tile([P, I], F32, name="zh", bufs=3)
+            product(zh[:], w1_codes[j][:], w1_scales[j][:], tab[:], tab_scales_g[:])
+            ht = ring.tile([P, I], F32, name="ht")
+            nc.scalar.activation(out=placed(ht[:]), in_=dealt(zh[:]), func=ACT.Tanh)
+            hw = ring.tile([P, I], BF16, name="hw", align_bytes=64)
+            nc.vector.scalar_tensor_tensor(out=hw[:], in0=ht[:], scalar=gain_col[:, j:j + 1], in1=vs_rows[:], op0=ALU.mult, op1=ALU.mult)
+            ht_grouped = ring.tile([P, P * PACK], BF16, name="ht_grouped", align_bytes=64)
+            turn_slots("ht", hw[:], ht_grouped[:])
+            n = [j in g for g in groups].index(True)
+            cols = slice((j - groups[n][0]) * P, (j - groups[n][0] + 1) * P)
+            quantize(ht_codes[n][:, cols], ht_scales[n][:, cols], ht_grouped[:])
+
+        for n, g in enumerate(groups):
+            width = len(g) * P
+            o_bank = ps.tile([P, I], F32, name="o_bank%d" % n, tag=("bank_b", "bank_a")[n % 2])
+            product(o_bank[:, :width], wt_codes[:], wt_scales[:], ht_codes[n][:], ht_scales[n][:])
+            result = sb.tile([P, width], F32, name="result%d" % n)
+            nc.scalar.copy(out=result[:], in_=o_bank[:, :width])
+            nc.sync.dma_start(out=out[:, g[0] * P:g[0] * P + width], in_=result[:])

@@ -19,8 +19,8 @@ ALU = mybir.AluOpType
 P = 128
 PACK = 4
 R_TILES = R // P
-W1_LOADS = 2
-CAST_ON_VECTOR = (0, 1)
+HALF = R // 2
+OUT_GROUPS = ((0, 1), (2,), (3,))
 
 
 def tile_attend_lrgained_asked_kernel(tc, query, query2, keys_words, keys_scales, tab_words, tab_scales,
@@ -28,9 +28,14 @@ def tile_attend_lrgained_asked_kernel(tc, query, query2, keys_words, keys_scales
     nc = tc.nc
     with ExitStack() as ctx:
         sb = ctx.enter_context(tc.tile_pool(name="sb", bufs=1))
-        ring = ctx.enter_context(tc.tile_pool(name="ring", bufs=2))
         ps = ctx.enter_context(tc.psum_pool(name="ps", bufs=1))
-        ps2 = ctx.enter_context(tc.psum_pool(name="ps2", bufs=2))
+        ps_products = ctx.enter_context(tc.psum_pool(name="ps_products", bufs=3))
+        ps_turned = ctx.enter_context(tc.psum_pool(name="ps_turned", bufs=2))
+
+        def load_rows(name, source, tag):
+            raw = sb.tile([P, PACK, source.shape[1]], F32, name=name, tag=tag)
+            nc.sync.dma_start(out=raw[:], in_=source.rearrange("(p t) c -> p t c", t=PACK))
+            return raw
 
         def load_words(name, words):
             window = sb.tile([P, T], U32, name=name, align_bytes=64)
@@ -41,146 +46,141 @@ def tile_attend_lrgained_asked_kernel(tc, query, query2, keys_words, keys_scales
             for row in range(4):
                 nc.sync.dma_start(out=window[row:P:32, :].bitcast(I32), in_=scales[0, row:16:4, :].bitcast(I32))
 
-        def gather(name, window, dtype):
-            picked = sb.tile([P, I], dtype, name=name, align_bytes=64)
+        def load_by_slot(name, vector):
+            column = sb.tile([P, PACK], F32, name=name)
+            nc.sync.dma_start(out=column[:], in_=vector.rearrange("o (p t) -> p (o t)", t=PACK))
+            return column
+
+        def gather(name, window, dtype, tag):
+            picked = sb.tile([P, I], dtype, name=name, tag=tag, align_bytes=64)
             nc.vector.tensor_copy(out=picked[:], in_=window[:].indirect(offsets[:]))
             return picked
 
-        def interleave(engine_copy, grouped, raw):
-            engine_copy(out=grouped.rearrange("p (c i) t -> p c t i", i=4), in_=raw.rearrange("p t (c i) -> p c t i", i=4))
+        def interleave(grouped, raw):
+            nc.scalar.copy(out=grouped.rearrange("p (c n t) -> p c t n", n=4, t=PACK), in_=raw[:].rearrange("p t (c n) -> p c t n", n=4))
 
-        def quantize(codes, scales, grouped):
-            nc.vector.quantize_mx(out=codes.bitcast(FP8X4), scales=scales, in_=grouped)
+        def quantize(name, grouped):
+            width = grouped.shape[1] // PACK
+            codes = sb.tile([P, width], U32, name=name + "_codes", align_bytes=64)
+            scales = sb.tile([P, width], U8, name=name + "_scales", align_bytes=64)
+            nc.vector.quantize_mx(out=codes[:].bitcast(FP8X4), scales=scales[:], in_=grouped)
+            return codes, scales
 
-        def product(bank, lhs, lhs_scales, rhs, rhs_scales):
-            nc.tensor.matmul_mx(out=bank, lhsT=lhs.bitcast(FP8X4), lhsT_scale=lhs_scales, rhs=rhs.bitcast(FP8X4),
-                                rhs_scale=rhs_scales, start=True, stop=True)
+        def product(bank, lhs, lhs_cols, rhs, rhs_cols):
+            nc.tensor.matmul_mx(out=bank, lhsT=lhs[0][:, lhs_cols].bitcast(FP8X4), lhsT_scale=lhs[1][:, lhs_cols],
+                                rhs=rhs[0][:, rhs_cols].bitcast(FP8X4), rhs_scale=rhs[1][:, rhs_cols], start=True, stop=True)
 
-        def turn_slots(name, values, grouped):
-            words = values.bitcast(F32)
-            turned = ps2.tile([P, 2, P], F32, name="turned")
-            for u in range(2):
-                nc.tensor.transpose(turned[:, u, :], words[:, u * P:(u + 1) * P], ident[:])
-            nc.scalar.copy(out=grouped.bitcast(F32).rearrange("p (c u) -> p c u", u=2), in_=turned[:].rearrange("p u c -> p c u"))
-
-        key_scale_window = sb.tile([P, T], U8, align_bytes=64)
-        tab_scale_window = sb.tile([P, T], U8, align_bytes=64)
-        nc.vector.memset(key_scale_window[:].bitcast(I32), 0)
-        nc.vector.memset(tab_scale_window[:].bitcast(I32), 0)
-
-        offsets = sb.tile([P, I // 16], U16)
-        nc.sync.dma_start(offsets[:], offs)
-        q2_raw = sb.tile([P, PACK, Q], F32)
-        nc.sync.dma_start(out=q2_raw[:], in_=query2.rearrange("(p t) q -> p t q", t=PACK))
-        q_raw = sb.tile([P, PACK, Q], F32)
-        nc.sync.dma_start(out=q_raw[:], in_=query.rearrange("(p t) q -> p t q", t=PACK))
-        load_scales(key_scale_window, keys_scales)
-        key_window = load_words("key_window", keys_words)
-        load_scales(tab_scale_window, tab_scales)
-        tab_window = load_words("tab_window", tab_words)
-        w1_cols = R // W1_LOADS
-        w1_raw = []
-        for h in range(W1_LOADS):
-            part = sb.tile([P, PACK, w1_cols], F32, name="w1_raw%d" % h)
-            nc.sync.dma_start(out=part[:], in_=w1[:, h * w1_cols:(h + 1) * w1_cols].rearrange("(p t) r -> p t r", t=PACK))
-            w1_raw.append(part)
-
-        ident = sb.tile([P, P], F32)
-        make_identity(nc, ident[:])
-        os_col = sb.tile([P, PACK], F32)
-        nc.gpsimd.dma_start(out=os_col[:], in_=slot_factor.rearrange("o (p t) -> p (o t)", t=PACK))
-        vs_col = sb.tile([P, PACK], F32)
-        nc.gpsimd.dma_start(out=vs_col[:], in_=vs.rearrange("o (p t) -> p (o t)", t=PACK))
-        gain_col = sb.tile([P, R_TILES], F32)
-        with nc.allow_non_contiguous_dma(reason="one gain a partition"):
-            nc.gpsimd.dma_start(out=gain_col[:], in_=gain.rearrange("(j m) o -> m (j o)", m=P))
-
-        warm = sb.tile([P, 1], F32)
-        nc.scalar.activation(out=warm[:], in_=ident[:, 0:1], func=ACT.Sigmoid)
-
-        os_rows = sb.tile([P, I], F32)
-        vs_rows = sb.tile([P, I], F32)
-        for rows, col in ((os_rows, os_col), (vs_rows, vs_col)):
-            spread = ps.tile([P, PACK, P], F32, name="spread")
-            for t in range(PACK):
-                nc.tensor.transpose(spread[:, t, :], col[:, t:t + 1].to_broadcast([P, P]), ident[:])
-            nc.scalar.copy(out=rows[:].rearrange("m (u s e) -> m u s e", u=2, e=2), in_=spread[:].rearrange("m (u e) s -> m u s e", u=2))
-
-        def dealt(bank):
+        def in_placed_order(bank):
             return bank.rearrange("m (s u e) -> m u s e", u=2, e=2)
 
         def placed(tile):
             return tile.rearrange("m (u s e) -> m u s e", u=2, e=2)
 
-        key_scales = gather("key_scales", key_scale_window, U8)
+        def spread(name, column, tag):
+            rows = ps.tile([P, I], F32, name=name, tag=tag)
+            for t in range(PACK):
+                nc.tensor.transpose(rows[:].rearrange("m (u s e) -> m u e s", u=2, e=2)[:, t // 2, t % 2, :],
+                                    column[:, t:t + 1].to_broadcast([P, P]), ident[:])
+            return rows
 
-        q_grouped = sb.tile([P, 2 * Q, PACK], BF16, align_bytes=64)
-        interleave(nc.scalar.copy, q_grouped[:, Q:, :], q2_raw[:])
-        interleave(nc.scalar.copy, q_grouped[:, :Q, :], q_raw[:])
-        q_codes = sb.tile([P, 2 * Q], U32, align_bytes=64)
-        q_scales = sb.tile([P, 2 * Q], U8, align_bytes=64)
-        quantize(q_codes[:], q_scales[:], q_grouped[:].rearrange("p c t -> p (c t)"))
+        def turn_slots(values, grouped):
+            words = values.bitcast(F32)
+            turned = ps_turned.tile([P, 2, P], F32)
+            for u in range(2):
+                nc.tensor.transpose(turned[:, u, :], words[:, u * P:(u + 1) * P], ident[:])
+            nc.scalar.copy(out=grouped.bitcast(F32).rearrange("s (c u) -> s c u", u=2), in_=turned[:].rearrange("s u c -> s c u"))
 
-        keys = gather("keys", key_window, U32)
+        everything = slice(None)
+
+        key_scale_window = sb.tile([P, T], U8, align_bytes=64)
+        nc.vector.memset(key_scale_window[:].bitcast(I32), 0)
+        zero = sb.tile([P, 1], F32, tag="expo")
+        nc.vector.memset(zero[:], 0.0)
+        table_preload = sb.tile([P, 1], F32)
+        nc.scalar.activation(out=table_preload[:], in_=zero[:], func=ACT.Sigmoid)
+        tab_scale_window = sb.tile([P, T], U8, align_bytes=64)
+        nc.vector.memset(tab_scale_window[:].bitcast(I32), 0)
+        ident = sb.tile([P, P], F32)
+        make_identity(nc, ident[:])
+
+        offsets = sb.tile([P, I // 16], U16)
+        nc.sync.dma_start(offsets[:], offs)
+        q2_raw = load_rows("q2_raw", query2, "q2_raw")
+        load_scales(key_scale_window, keys_scales)
+        q_raw = load_rows("q_raw", query, "q_raw")
+        key_window = load_words("key_window", keys_words)
+        load_scales(tab_scale_window, tab_scales)
+        os_column = load_by_slot("os_column", slot_factor)
+        vs_column = load_by_slot("vs_column", vs)
+        w1_raw0 = load_rows("w1_raw0", w1[:, :HALF], "gate")
+        tab_window = load_words("tab_window", tab_words)
+        w1_raw1 = load_rows("w1_raw1", w1[:, HALF:], "w1_raw1")
+        gain_column = sb.tile([P, R_TILES], F32)
+        with nc.allow_non_contiguous_dma(reason="gain[128 j + m] goes to partition m, column j"):
+            nc.sync.dma_start(out=gain_column[:], in_=gain.rearrange("(j m) o -> m (j o)", m=P))
+
+        key_scales = gather("key_scales", key_scale_window, U8, "key_scales")
+        q_grouped = sb.tile([P, 2 * Q * PACK], BF16, align_bytes=64)
+        interleave(q_grouped[:, Q * PACK:], q2_raw)
+        interleave(q_grouped[:, :Q * PACK], q_raw)
+        q_mx = quantize("q", q_grouped[:])
+        key_codes = gather("key_codes", key_window, U32, "picked_words")
         b_bank = ps.tile([P, I], F32, tag="bank_b")
-        product(b_bank[:], q_codes[:, Q:], q_scales[:, Q:], keys[:], key_scales[:])
-        a_bank = ps.tile([P, I], F32, tag="bank_a")
-        product(a_bank[:], q_codes[:, :Q], q_scales[:, :Q], keys[:], key_scales[:])
+        product(b_bank[:], q_mx, slice(Q, 2 * Q), (key_codes, key_scales), everything)
+        a_bank = ps.tile([P, I], F32)
+        product(a_bank[:], q_mx, slice(0, Q), (key_codes, key_scales), everything)
 
+        tab_scale_bytes = gather("tab_scale_bytes", tab_scale_window, U8, "key_window")
+        w1_grouped0 = sb.tile([P, HALF * PACK], BF16, align_bytes=64)
+        interleave(w1_grouped0[:], w1_raw0)
         gate = sb.tile([P, I], F32)
-        nc.scalar.activation(out=placed(gate[:]), in_=dealt(b_bank[:]), func=ACT.Sigmoid)
-        tab_scales_g = gather("tab_scales_g", tab_scale_window, U8)
+        nc.scalar.activation(out=placed(gate[:]), in_=in_placed_order(b_bank[:]), func=ACT.Sigmoid, bias=zero[:])
         neg_max = sb.tile([P, 1], F32)
         nc.vector.tensor_reduce(out=neg_max[:], in_=a_bank[:], axis=mybir.AxisListType.X, op=ALU.max, negate=True)
+        w1_mx0 = quantize("w1_0", w1_grouped0[:])
+        os_rows = spread("os_rows", os_column, "bank_b")
+        vs_rows = spread("vs_rows", vs_column, "bank_vs")
         expo = sb.tile([P, I], F32)
-        nc.scalar.activation(out=placed(expo[:]), in_=dealt(a_bank[:]), func=ACT.Exp, bias=neg_max[:])
-        tab = gather("tab", tab_window, U32)
+        nc.scalar.activation(out=placed(expo[:]), in_=in_placed_order(a_bank[:]), func=ACT.Exp, bias=neg_max[:])
+        tab_codes = gather("tab_codes", tab_window, U32, "picked_words")
+        w1_grouped1 = sb.tile([P, HALF * PACK], BF16, align_bytes=64)
+        interleave(w1_grouped1[:], w1_raw1)
 
-        prob = sb.tile([P, I], F32)
+        prob = sb.tile([P, I], F32, tag="tab_window", align_bytes=64)
         total = sb.tile([P, 1], F32)
         nc.vector.scalar_tensor_tensor(out=prob[:], in0=expo[:], scalar=1.0, in1=gate[:], op0=ALU.mult, op1=ALU.mult,
                                        accum_out=total[:])
+        w1_mx1 = quantize("w1_1", w1_grouped1[:])
         inv_total = sb.tile([P, 1], F32)
         nc.vector.reciprocal(out=inv_total[:], in_=total[:])
         weights = sb.tile([P, I], BF16, align_bytes=64)
         nc.vector.scalar_tensor_tensor(out=weights[:], in0=prob[:], scalar=inv_total[:], in1=os_rows[:], op0=ALU.mult, op1=ALU.mult)
         wt_grouped = sb.tile([P, Q * PACK], BF16, align_bytes=64)
-        turn_slots("wt", weights[:], wt_grouped[:])
-        wt_codes = sb.tile([P, Q], U32, align_bytes=64)
-        wt_scales = sb.tile([P, Q], U8, align_bytes=64)
-        quantize(wt_codes[:], wt_scales[:], wt_grouped[:])
+        turn_slots(weights[:], wt_grouped[:])
+        wt_mx = quantize("wt", wt_grouped[:])
 
-        per_load = R_TILES // W1_LOADS
-        groups = ((0, 1), (2,), (3,))
-        ht_codes = [sb.tile([P, len(g) * P], U32, name="ht_codes%d" % n, align_bytes=64) for n, g in enumerate(groups)]
-        ht_scales = [sb.tile([P, len(g) * P], U8, name="ht_scales%d" % n, align_bytes=64) for n, g in enumerate(groups)]
-        w1_codes = []
-        w1_scales = []
+        ht = []
         for j in range(R_TILES):
-            cols = slice((j % per_load) * P, (j % per_load + 1) * P)
-            w1_grouped = sb.tile([P, P, PACK], BF16, name="w1_grouped%d" % j, align_bytes=64)
-            interleave(nc.vector.tensor_copy if j in CAST_ON_VECTOR else nc.scalar.copy, w1_grouped[:], w1_raw[j // per_load][:, :, cols])
-            w1_codes.append(sb.tile([P, P], U32, name="w1_codes%d" % j, align_bytes=64))
-            w1_scales.append(sb.tile([P, P], U8, name="w1_scales%d" % j, align_bytes=64))
-            quantize(w1_codes[j][:], w1_scales[j][:], w1_grouped[:].rearrange("p c t -> p (c t)"))
+            zh = ps_products.tile([P, I], F32, name="product_bank")
+            first = j * P % HALF
+            product(zh[:], (w1_mx0, w1_mx1)[j * P // HALF], slice(first, first + P), (tab_codes, tab_scale_bytes), everything)
+            ht.append(sb.tile([P, I], F32, name="ht%d" % j))
+            nc.scalar.activation(out=placed(ht[j][:]), in_=in_placed_order(zh[:]), func=ACT.Tanh)
+        ht_grouped = [sb.tile([P, len(group) * P * PACK], BF16, name="ht_grouped%d" % n, align_bytes=64)
+                      for n, group in enumerate(OUT_GROUPS)]
+        for n, group in enumerate(OUT_GROUPS):
+            for j in group:
+                hw = sb.tile([P, I], BF16, name="hw%d" % j, align_bytes=64)
+                nc.vector.scalar_tensor_tensor(out=hw[:], in0=ht[j][:], scalar=gain_column[:, j:j + 1], in1=vs_rows[:],
+                                               op0=ALU.mult, op1=ALU.mult)
+                place = (j - group[0]) * P * PACK
+                turn_slots(hw[:], ht_grouped[n][:, place:place + P * PACK])
+        ht_mx = [quantize("ht_group%d" % n, ht_grouped[n][:]) for n in range(len(OUT_GROUPS))]
 
-        for j in range(R_TILES):
-            zh = ps2.tile([P, I], F32, name="zh", bufs=3)
-            product(zh[:], w1_codes[j][:], w1_scales[j][:], tab[:], tab_scales_g[:])
-            ht = ring.tile([P, I], F32, name="ht")
-            nc.scalar.activation(out=placed(ht[:]), in_=dealt(zh[:]), func=ACT.Tanh)
-            hw = ring.tile([P, I], BF16, name="hw", align_bytes=64)
-            nc.vector.scalar_tensor_tensor(out=hw[:], in0=ht[:], scalar=gain_col[:, j:j + 1], in1=vs_rows[:], op0=ALU.mult, op1=ALU.mult)
-            ht_grouped = ring.tile([P, P * PACK], BF16, name="ht_grouped", align_bytes=64)
-            turn_slots("ht", hw[:], ht_grouped[:])
-            n = [j in g for g in groups].index(True)
-            cols = slice((j - groups[n][0]) * P, (j - groups[n][0] + 1) * P)
-            quantize(ht_codes[n][:, cols], ht_scales[n][:, cols], ht_grouped[:])
-
-        for n, g in enumerate(groups):
-            width = len(g) * P
-            o_bank = ps.tile([P, I], F32, name="o_bank%d" % n, tag=("bank_b", "bank_a")[n % 2])
-            product(o_bank[:, :width], wt_codes[:], wt_scales[:], ht_codes[n][:], ht_scales[n][:])
+        for n, group in enumerate(OUT_GROUPS):
+            width = len(group) * P
+            o_bank = ps_products.tile([P, I], F32, name="product_bank")
+            product(o_bank[:, :width], wt_mx, everything, ht_mx[n], everything)
             result = sb.tile([P, width], F32, name="result%d" % n)
             nc.scalar.copy(out=result[:], in_=o_bank[:, :width])
-            nc.sync.dma_start(out=out[:, g[0] * P:g[0] * P + width], in_=result[:])
+            nc.sync.dma_start(out=out[:, group[0] * P:group[0] * P + width], in_=result[:])

from contextlib import ExitStack

import concourse.mybir as mybir
from concourse.masks import make_identity

D, K, R, T, I, Q = 512, 512, 512, 2048, 512, 128
FLOPS = 2 * (2 * D * Q * I + K * R * I + I * Q * R)

F32 = mybir.dt.float32
BF16 = mybir.dt.bfloat16
I32 = mybir.dt.int32
U32 = mybir.dt.uint32
U16 = mybir.dt.uint16
U8 = mybir.dt.uint8
FP8X4 = mybir.dt.float8_e4m3fn_x4
ACT = mybir.ActivationFunctionType
ALU = mybir.AluOpType

P = 128
PACK = 4
R_TILES = R // P
HALF = R // 2
OUT_GROUPS = ((0, 1), (2,), (3,))


def tile_attend_lrgained_asked_kernel(tc, query, query2, keys_words, keys_scales, tab_words, tab_scales,
                                       w1, gain, slot_factor, vs, offs, out):
    nc = tc.nc
    with ExitStack() as ctx:
        sb = ctx.enter_context(tc.tile_pool(name="sb", bufs=1))
        ps = ctx.enter_context(tc.psum_pool(name="ps", bufs=1))
        ps_products = ctx.enter_context(tc.psum_pool(name="ps_products", bufs=3))
        ps_turned = ctx.enter_context(tc.psum_pool(name="ps_turned", bufs=2))

        def load_rows(name, source, tag):
            raw = sb.tile([P, PACK, source.shape[1]], F32, name=name, tag=tag)
            nc.sync.dma_start(out=raw[:], in_=source.rearrange("(p t) c -> p t c", t=PACK))
            return raw

        def load_words(name, words):
            window = sb.tile([P, T], U32, name=name, align_bytes=64)
            nc.sync.dma_start(out=window[:].bitcast(I32), in_=words[0].rearrange("p n t -> p (n t)").bitcast(I32))
            return window

        def load_scales(window, scales):
            for row in range(4):
                nc.sync.dma_start(out=window[row:P:32, :].bitcast(I32), in_=scales[0, row:16:4, :].bitcast(I32))

        def load_by_slot(name, vector):
            column = sb.tile([P, PACK], F32, name=name)
            nc.sync.dma_start(out=column[:], in_=vector.rearrange("o (p t) -> p (o t)", t=PACK))
            return column

        def gather(name, window, dtype, tag):
            picked = sb.tile([P, I], dtype, name=name, tag=tag, align_bytes=64)
            nc.vector.tensor_copy(out=picked[:], in_=window[:].indirect(offsets[:]))
            return picked

        def interleave(grouped, raw):
            nc.scalar.copy(out=grouped.rearrange("p (c n t) -> p c t n", n=4, t=PACK), in_=raw[:].rearrange("p t (c n) -> p c t n", n=4))

        def quantize(name, grouped):
            width = grouped.shape[1] // PACK
            codes = sb.tile([P, width], U32, name=name + "_codes", align_bytes=64)
            scales = sb.tile([P, width], U8, name=name + "_scales", align_bytes=64)
            nc.vector.quantize_mx(out=codes[:].bitcast(FP8X4), scales=scales[:], in_=grouped)
            return codes, scales

        def product(bank, lhs, lhs_cols, rhs, rhs_cols):
            nc.tensor.matmul_mx(out=bank, lhsT=lhs[0][:, lhs_cols].bitcast(FP8X4), lhsT_scale=lhs[1][:, lhs_cols],
                                rhs=rhs[0][:, rhs_cols].bitcast(FP8X4), rhs_scale=rhs[1][:, rhs_cols], start=True, stop=True)

        def in_placed_order(bank):
            return bank.rearrange("m (s u e) -> m u s e", u=2, e=2)

        def placed(tile):
            return tile.rearrange("m (u s e) -> m u s e", u=2, e=2)

        def spread(name, column, tag):
            rows = ps.tile([P, I], F32, name=name, tag=tag)
            for t in range(PACK):
                nc.tensor.transpose(rows[:].rearrange("m (u s e) -> m u e s", u=2, e=2)[:, t // 2, t % 2, :],
                                    column[:, t:t + 1].to_broadcast([P, P]), ident[:])
            return rows

        def turn_slots(values, grouped):
            words = values.bitcast(F32)
            turned = ps_turned.tile([P, 2, P], F32)
            for u in range(2):
                nc.tensor.transpose(turned[:, u, :], words[:, u * P:(u + 1) * P], ident[:])
            nc.scalar.copy(out=grouped.bitcast(F32).rearrange("s (c u) -> s c u", u=2), in_=turned[:].rearrange("s u c -> s c u"))

        everything = slice(None)

        key_scale_window = sb.tile([P, T], U8, align_bytes=64)
        nc.vector.memset(key_scale_window[:].bitcast(I32), 0)
        zero = sb.tile([P, 1], F32, tag="expo")
        nc.vector.memset(zero[:], 0.0)
        table_preload = sb.tile([P, 1], F32)
        nc.scalar.activation(out=table_preload[:], in_=zero[:], func=ACT.Sigmoid)
        tab_scale_window = sb.tile([P, T], U8, align_bytes=64)
        nc.vector.memset(tab_scale_window[:].bitcast(I32), 0)
        ident = sb.tile([P, P], F32)
        make_identity(nc, ident[:])

        offsets = sb.tile([P, I // 16], U16)
        nc.sync.dma_start(offsets[:], offs)
        q2_raw = load_rows("q2_raw", query2, "q2_raw")
        load_scales(key_scale_window, keys_scales)
        q_raw = load_rows("q_raw", query, "q_raw")
        key_window = load_words("key_window", keys_words)
        load_scales(tab_scale_window, tab_scales)
        os_column = load_by_slot("os_column", slot_factor)
        vs_column = load_by_slot("vs_column", vs)
        w1_raw0 = load_rows("w1_raw0", w1[:, :HALF], "gate")
        tab_window = load_words("tab_window", tab_words)
        w1_raw1 = load_rows("w1_raw1", w1[:, HALF:], "w1_raw1")
        gain_column = sb.tile([P, R_TILES], F32)
        with nc.allow_non_contiguous_dma(reason="gain[128 j + m] goes to partition m, column j"):
            nc.sync.dma_start(out=gain_column[:], in_=gain.rearrange("(j m) o -> m (j o)", m=P))

        key_scales = gather("key_scales", key_scale_window, U8, "key_scales")
        q_grouped = sb.tile([P, 2 * Q * PACK], BF16, align_bytes=64)
        interleave(q_grouped[:, Q * PACK:], q2_raw)
        interleave(q_grouped[:, :Q * PACK], q_raw)
        q_mx = quantize("q", q_grouped[:])
        key_codes = gather("key_codes", key_window, U32, "picked_words")
        b_bank = ps.tile([P, I], F32, tag="bank_b")
        product(b_bank[:], q_mx, slice(Q, 2 * Q), (key_codes, key_scales), everything)
        a_bank = ps.tile([P, I], F32)
        product(a_bank[:], q_mx, slice(0, Q), (key_codes, key_scales), everything)

        tab_scale_bytes = gather("tab_scale_bytes", tab_scale_window, U8, "key_window")
        w1_grouped0 = sb.tile([P, HALF * PACK], BF16, align_bytes=64)
        interleave(w1_grouped0[:], w1_raw0)
        gate = sb.tile([P, I], F32)
        nc.scalar.activation(out=placed(gate[:]), in_=in_placed_order(b_bank[:]), func=ACT.Sigmoid, bias=zero[:])
        neg_max = sb.tile([P, 1], F32)
        nc.vector.tensor_reduce(out=neg_max[:], in_=a_bank[:], axis=mybir.AxisListType.X, op=ALU.max, negate=True)
        w1_mx0 = quantize("w1_0", w1_grouped0[:])
        os_rows = spread("os_rows", os_column, "bank_b")
        vs_rows = spread("vs_rows", vs_column, "bank_vs")
        expo = sb.tile([P, I], F32)
        nc.scalar.activation(out=placed(expo[:]), in_=in_placed_order(a_bank[:]), func=ACT.Exp, bias=neg_max[:])
        tab_codes = gather("tab_codes", tab_window, U32, "picked_words")
        w1_grouped1 = sb.tile([P, HALF * PACK], BF16, align_bytes=64)
        interleave(w1_grouped1[:], w1_raw1)

        prob = sb.tile([P, I], F32, tag="tab_window", align_bytes=64)
        total = sb.tile([P, 1], F32)
        nc.vector.scalar_tensor_tensor(out=prob[:], in0=expo[:], scalar=1.0, in1=gate[:], op0=ALU.mult, op1=ALU.mult,
                                       accum_out=total[:])
        w1_mx1 = quantize("w1_1", w1_grouped1[:])
        inv_total = sb.tile([P, 1], F32)
        nc.vector.reciprocal(out=inv_total[:], in_=total[:])
        weights = sb.tile([P, I], BF16, align_bytes=64)
        nc.vector.scalar_tensor_tensor(out=weights[:], in0=prob[:], scalar=inv_total[:], in1=os_rows[:], op0=ALU.mult, op1=ALU.mult)
        wt_grouped = sb.tile([P, Q * PACK], BF16, align_bytes=64)
        turn_slots(weights[:], wt_grouped[:])
        wt_mx = quantize("wt", wt_grouped[:])

        ht = []
        for j in range(R_TILES):
            zh = ps_products.tile([P, I], F32, name="product_bank")
            first = j * P % HALF
            product(zh[:], (w1_mx0, w1_mx1)[j * P // HALF], slice(first, first + P), (tab_codes, tab_scale_bytes), everything)
            ht.append(sb.tile([P, I], F32, name="ht%d" % j))
            nc.scalar.activation(out=placed(ht[j][:]), in_=in_placed_order(zh[:]), func=ACT.Tanh)
        ht_grouped = [sb.tile([P, len(group) * P * PACK], BF16, name="ht_grouped%d" % n, align_bytes=64)
                      for n, group in enumerate(OUT_GROUPS)]
        for n, group in enumerate(OUT_GROUPS):
            for j in group:
                hw = sb.tile([P, I], BF16, name="hw%d" % j, align_bytes=64)
                nc.vector.scalar_tensor_tensor(out=hw[:], in0=ht[j][:], scalar=gain_column[:, j:j + 1], in1=vs_rows[:],
                                               op0=ALU.mult, op1=ALU.mult)
                place = (j - group[0]) * P * PACK
                turn_slots(hw[:], ht_grouped[n][:, place:place + P * PACK])
        ht_mx = [quantize("ht_group%d" % n, ht_grouped[n][:]) for n in range(len(OUT_GROUPS))]

        for n, group in enumerate(OUT_GROUPS):
            width = len(group) * P
            o_bank = ps_products.tile([P, I], F32, name="product_bank")
            product(o_bank[:, :width], wt_mx, everything, ht_mx[n], everything)
            result = sb.tile([P, width], F32, name="result%d" % n)
            nc.scalar.copy(out=result[:], in_=o_bank[:, :width])
            nc.sync.dma_start(out=out[:, group[0] * P:group[0] * P + width], in_=result[:])
